import numpy as np
import ml_dtypes


def mxq(x, axis, fmt="e4m3"):
    dtype, down = {"e4m3": (ml_dtypes.float8_e4m3fn, 7), "e5m2": (ml_dtypes.float8_e5m2, 14)}[fmt]
    v = np.moveaxis(np.asarray(x, np.float32).astype(ml_dtypes.bfloat16).astype(np.float64), axis, -1)
    blocks = v.reshape(v.shape[:-1] + (-1, 32))
    amax = np.abs(blocks).max(-1, keepdims=True)
    byte = np.maximum(np.where(amax > 0, np.frexp(amax)[1] - 1 + 127, 0) - down, 1)
    scale = np.exp2(byte - 127.0)
    codes = (blocks / scale).astype(np.float32).astype(dtype).astype(np.float64)
    return np.moveaxis((codes * scale).reshape(v.shape), -1, axis)


WIDE = False


def mx_kscale(k):
    if not WIDE:
        return np.ones(k)
    levels = np.array([10, -10, 5, -5, 0])
    if k % 512:
        return np.exp2(np.random.permutation(np.resize(levels, k // 32))).repeat(32)
    a = np.empty((k // 512, 16))
    for p in range(k // 512):
        a[p, :8] = np.random.permutation(np.resize(levels, 8))
        for g in range(8):
            far = levels[np.abs(levels - a[p, g]) >= 10]
            a[p, g + 8] = far[np.random.randint(len(far))]
    return np.exp2(a.ravel()).repeat(32)


def f64(x):
    return np.asarray(x).astype(np.float64)


def striped(idx):
    return np.tile(idx.reshape(-1, 16).T, (8, 1)).astype(np.uint16)


def unstriped(offs):
    return offs[:16].T.reshape(-1).astype(np.int64)


E2M1 = np.array([0.0, 0.5, 1.0, 1.5, 2.0, 3.0, 4.0, 6.0, -0.0, -0.5, -1.0, -1.5, -2.0, -3.0, -4.0, -6.0])


def pack_weight(w, fmt):
    k, n = w.shape
    w = f64(np.asarray(w, np.float32).astype(ml_dtypes.bfloat16)).reshape(k // 32, 32, n)
    amax = np.abs(w).max(1)
    if fmt == "e4m3":
        byte = np.frexp(amax)[1] - 1 + 127 - 7
    else:
        mant, ex = np.frexp(amax / 6.0)
        byte = np.where(mant > 0.5, ex, ex - 1) + 127
    byte = np.clip(np.where(amax > 0, byte, 1), 1, 254)
    scaled = (w * np.exp2(127.0 - byte)[:, None, :]).reshape(k, n).astype(np.float32)
    by_word = np.ascontiguousarray(scaled.reshape(k // 512, 128, 4, n).transpose(0, 1, 3, 2))
    if fmt == "e4m3":
        words = by_word.astype(ml_dtypes.float8_e4m3fn).view(np.uint8)
    else:
        c = by_word.astype(ml_dtypes.float4_e2m1fn).view(np.uint8) & 0xF
        words = (c[..., 0::2] | (c[..., 1::2] << 4)).reshape(k // 512, 128, 2 * n)
    return np.ascontiguousarray(words), np.ascontiguousarray(byte.astype(np.uint8).reshape(k // 512, 16, n))


def unpack_weight(words, scales, fmt):
    g, _, n = scales.shape
    words = np.ascontiguousarray(words).reshape(g, 128, n, -1)
    if fmt == "e4m3":
        vals = words.view(ml_dtypes.float8_e4m3fn).astype(np.float64)
    else:
        nib = np.empty((g, 128, n, 4), np.uint8)
        nib[..., 0::2] = words & 0xF
        nib[..., 1::2] = words >> 4
        vals = E2M1[nib]
    vals = vals * np.repeat(np.exp2(scales.astype(np.float64) - 127.0), 8, axis=1)[..., None]
    return vals.transpose(0, 1, 3, 2).reshape(g * 512, n)


def gelu(v):
    return 0.5 * v * (1.0 + np.tanh(np.sqrt(2.0 / np.pi) * (v + 0.044715 * v**3)))


def striped8(idx):
    return np.concatenate([v.reshape(-1, 16).T for v in idx]).astype(np.uint16)


def unstriped8(offs):
    return np.stack([offs[16 * g:16 * g + 16].T.reshape(-1) for g in range(8)]).astype(np.int64)


def heads(h, wgt, idx8):
    r = np.arange(h.shape[0])
    return wgt[r // 4 % 128] * h[r[:, None], idx8[r % 512 // 64]]


def put_heads(h, wgs, idx8, t2):
    r = np.arange(h.shape[0])
    page = np.zeros((h.shape[0], t2))
    page[r[:, None], idx8[r % 512 // 64]] = wgs[r // 4 % 128] * h
    return page


K, H, N, T, S, P, T2 = 512, 1024, 1024, 4096, 1024, 512, 1024

def setup_inputs():
    n = np.random.standard_normal
    s = mx_kscale(K)[:, None]
    u = mx_kscale(H)[:, None]
    d = {}
    d["tab_words"], d["tab_scales"] = pack_weight(n((K, T)) * s, "e4m3")
    d["offs"] = striped(np.random.permutation(T)[:S])
    d["w1"] = (1.2 * n((K, H)) / K**0.5 / s).astype(np.float32)
    d["w2_words"], d["w2_scales"] = pack_weight(1.8 * n((K, H)) / K**0.5 / s, "e2m1")
    d["offs2"] = striped8(np.stack([np.random.permutation(S)[:P] for _ in range(8)]))
    d["wgt"] = np.repeat(np.random.uniform(0.5, 2.0, (8, P)), 16, axis=0).astype(np.float32)
    d["sens"] = (np.exp(0.3 * n(H)) * u[:, 0]).astype(np.float32)
    d["w3"] = (0.5 * n((H, N)) / H**0.5 / u).astype(np.float32)
    d["w4_words"], d["w4_scales"] = pack_weight(0.5 * n((H, N)) / H**0.5 / u, "e4m3")
    d["gain"] = np.exp(0.3 * n(N)).astype(np.float32)
    d["offs3"] = striped8(np.stack([np.random.permutation(T2)[:P] for _ in range(8)]))
    d["wgo"] = np.repeat(np.random.uniform(0.5, 2.0, (8, P)), 16, axis=0).astype(np.float32)
    return d

def reference(tab_words, tab_scales, offs, w1, w2_words, w2_scales, offs2, wgt, sens, w3, w4_words, w4_scales, gain, offs3, wgo):
    v = unpack_weight(tab_words, tab_scales, "e4m3")[:, unstriped(offs)]
    a = mxq(f64(w1), 0, "e4m3").T @ v
    b = unpack_weight(w2_words, w2_scales, "e2m1").T @ v
    h = np.maximum(a, b * np.tanh(a))
    x = heads(h, f64(wgt), unstriped8(offs2)) * f64(sens)[:, None]
    xq = mxq(x, 0, "e4m3")
    e1 = mxq(f64(w3), 0, "e4m3").T @ xq
    e2 = unpack_weight(w4_words, w4_scales, "e4m3").T @ xq
    y = np.square(e1 - e2) * f64(gain)[:, None]
    return put_heads(y, f64(wgo), unstriped8(offs3), T2)

@@ -1,0 +1,243 @@
+from contextlib import ExitStack
+
+import concourse.mybir as mybir
+
+K, H, N, T, S, M, T2 = 512, 1024, 1024, 4096, 1024, 512, 1024
+FLOPS = 2 * (2 * K * H * S + 2 * H * N * M)
+
+F32 = mybir.dt.float32
+BF16 = mybir.dt.bfloat16
+I32 = mybir.dt.int32
+U32 = mybir.dt.uint32
+U16 = mybir.dt.uint16
+U8 = mybir.dt.uint8
+FP8X4 = mybir.dt.float8_e4m3fn_x4
+FP4X4 = mybir.dt.float4_e2m1fn_x4
+ACT = mybir.ActivationFunctionType
+ALU = mybir.AluOpType
+
+P = 128
+PACK = 4
+BLK = P * PACK
+BANK = 512
+PAGES = 4
+
+
+def tile_list_sapline_leak_ledger_kernel(
+    tc, tab_words, tab_scales, offs, w1, w2_words, w2_scales, offs2, wgt, sens, w3, w4_words, w4_scales, gain, offs3, wgo, out
+):
+    nc = tc.nc
+    with ExitStack() as ctx:
+        keep = ctx.enter_context(tc.tile_pool(name="keep", bufs=1))
+        work = ctx.enter_context(tc.tile_pool(name="work", bufs=2))
+        psum = ctx.enter_context(tc.psum_pool(name="psum", bufs=4))
+
+        def load_scale_rows(queue, plane, first, rows):
+            n = rows.shape[0] * 4
+            for q in range(4):
+                queue.dma_start(
+                    out=plane[32 * q + first : 32 * q + first + n, :].bitcast(I32),
+                    in_=rows[:, 4 * q : 4 * q + 4, :].bitcast(I32),
+                )
+
+        def deal(dst, src):
+            nc.vector.tensor_copy(
+                out=dst.rearrange("p (c t m) -> p c m t", t=PACK, m=P),
+                in_=src.rearrange("p (c m t) -> p c m t", t=PACK, m=P),
+            )
+
+        def load_weight(w, a, c):
+            raw = work.tile([P, PACK, BLK], F32, name="raw", tag="raw")
+            nc.sync.dma_start(
+                out=raw[:], in_=w[BLK * a : BLK * (a + 1), BLK * c : BLK * (c + 1)].rearrange("(p j) n -> p j n", j=PACK)
+            )
+            return raw
+
+        def round_weight(raw, sign):
+            grouped = work.tile([P, PACK, P, PACK], BF16, name="grouped", tag="grouped", align_bytes=64)
+            for half in range(2):
+                ms = slice(64 * half, 64 * half + 64)
+                nc.scalar.activation(
+                    out=grouped[:].rearrange("p t m j -> p m j t")[:, ms],
+                    in_=raw[:].rearrange("p j (m t) -> p m j t", t=PACK)[:, ms],
+                    func=ACT.Copy,
+                    scale=sign,
+                )
+            return grouped
+
+        def quantize(grouped, name):
+            codes = keep.tile([P, BLK], U32, name=name + "_codes", align_bytes=64)
+            scales = keep.tile([P, BLK], U8, name=name + "_scales", align_bytes=64)
+            nc.vector.quantize_mx(out=codes[:].bitcast(FP8X4), scales=scales[:], in_=grouped)
+            return codes, scales
+
+        def flat4(grouped):
+            return grouped[:].rearrange("p t m j -> p (t m j)")
+
+        def scaled_rows(rows, col, tag):
+            t = work.tile([P, M], F32, name=tag, tag=tag, bufs=4)
+            nc.scalar.activation(out=t[:], in_=rows[:], func=ACT.Copy, scale=col)
+            return t
+
+        list1 = keep.tile([P, S // 16], U16, name="list1")
+        list2 = keep.tile([P, M // 16], U16, name="list2")
+        list3 = keep.tile([P, M // 16], U16, name="list3")
+        tab_s = keep.tile([P, T], U8, name="tab_s", align_bytes=64)
+        w2_s_raw = keep.tile([P, H], U8, name="w2_s_raw", align_bytes=64)
+        w4_s_raw = keep.tile([P, N], U8, name="w4_s_raw", align_bytes=64)
+        nc.vector.memset(tab_s[:].bitcast(I32), 0)
+        nc.vector.memset(w2_s_raw[:].bitcast(I32), 0)
+        nc.vector.memset(w4_s_raw[:].bitcast(I32), 0)
+
+        nc.sync.dma_start(list1[:], offs)
+        w1_raw0 = load_weight(w1, 0, 0)
+        load_scale_rows(nc.sync, tab_s, 0, tab_scales)
+        w2_raw = keep.tile([P, 2 * H], U8, name="w2_raw", align_bytes=64)
+        nc.sync.dma_start(out=w2_raw[:].bitcast(I32), in_=w2_words[0].bitcast(I32))
+        tab_w = keep.tile([P, T], I32, name="tab_w", align_bytes=64)
+        nc.sync.dma_start(out=tab_w[:], in_=tab_words[0].rearrange("p t i -> p (t i)").bitcast(I32))
+        load_scale_rows(nc.sync, w2_s_raw, 0, w2_scales)
+        nc.sync.dma_start(list2[:], offs2)
+        wgt_t = keep.tile([P, M], F32, name="wgt_t")
+        nc.sync.dma_start(out=wgt_t[:], in_=wgt)
+        sens_t = keep.tile([P, H // BLK, PACK], F32, name="sens_t")
+        nc.sync.dma_start(out=sens_t[:], in_=sens.rearrange("(b p i) -> p b i", p=P, i=PACK))
+        w1_raw1 = load_weight(w1, 0, 1)
+
+        v_s = keep.tile([P, S], U8, name="v_s", align_bytes=64)
+        nc.vector.tensor_copy(v_s[:], tab_s[:].indirect(list1[:]))
+        w2_w = keep.tile([P, 2 * H], U8, name="w2_w", align_bytes=64)
+        w2_s = keep.tile([P, H], U8, name="w2_s", align_bytes=64)
+        deal(w2_w[:].bitcast(U16), w2_raw[:].bitcast(U16))
+        w1_q = [quantize(flat4(round_weight(w1_raw0, 1.0)), "w1_0")]
+        v_w = []
+        for half in range(S // BANK):
+            vw = keep.tile([P, BANK], U32, name="v_w%d" % half, align_bytes=64)
+            nc.vector.tensor_copy(vw[:], tab_w[:].bitcast(U32).indirect(list1[:, 32 * half : 32 * half + 32]))
+            v_w.append(vw)
+            if half == 0:
+                deal(w2_s[:], w2_s_raw[:])
+        pages = []
+        for k in range(PAGES):
+            page = keep.tile([P, T2], F32, name="page%d" % k)
+            nc.vector.memset(page[:], 0.0)
+            pages.append(page)
+
+        w3_q = {}
+        w3_grouped = {}
+        w4_raw = []
+        x_q = []
+        picked = {}
+        pending = []
+
+        def gather(b, i, h, ws):
+            if i == 0:
+                picked[b] = work.tile([P, PACK, M], F32, name="picked", tag="picked")
+            nc.vector.tensor_tensor(picked[b][:, i, :], h[:].indirect(list2[:]), ws[:], ALU.mult)
+
+        def round_x(b, parts):
+            xb = work.tile([P, M, PACK], BF16, name="xb", tag="xb", align_bytes=64)
+            for copy, cs in parts:
+                copy(
+                    out=xb[:].rearrange("p (c e) i -> p c i e", e=4)[:, cs],
+                    in_=picked[b][:].rearrange("p i (c e) -> p c i e", e=4)[:, cs],
+                )
+            return xb
+
+        for b in range(H // BLK):
+            for i in range(PACK):
+                cols = slice(P * i, P * (i + 1))
+                w2_cols = slice(BLK * b + P * i, BLK * b + P * (i + 1))
+                w2_bytes = slice(2 * (BLK * b + P * i), 2 * (BLK * b + P * (i + 1)))
+                a_ps, b_ps, th = [], [], []
+                for half in range(S // BANK):
+                    js = slice(BANK * half, BANK * (half + 1))
+                    pa = psum.tile([P, BANK], F32, name="pa", tag="pa")
+                    pb = psum.tile([P, BANK], F32, name="pb", tag="pb")
+                    nc.tensor.matmul_mx(
+                        out=pa[:], lhsT=w1_q[b][0][:, cols].bitcast(FP8X4), lhsT_scale=w1_q[b][1][:, cols],
+                        rhs=v_w[half][:].bitcast(FP8X4), rhs_scale=v_s[:, js], start=True, stop=True,
+                    )
+                    nc.tensor.matmul_mx(
+                        out=pb[:], lhsT=w2_w[:, w2_bytes].bitcast(FP4X4), lhsT_scale=w2_s[:, w2_cols],
+                        rhs=v_w[half][:].bitcast(FP8X4), rhs_scale=v_s[:, js], start=True, stop=True,
+                    )
+                    t = work.tile([P, BANK], F32, name="tanh_a", tag="tanh_a", bufs=4)
+                    nc.scalar.activation(out=t[:], in_=pa[:], func=ACT.Tanh)
+                    a_ps.append(pa)
+                    b_ps.append(pb)
+                    th.append(t)
+                ws = scaled_rows(wgt_t, sens_t[:, b, i : i + 1], "ws")
+                h = work.tile([P, S], F32, name="h", tag="h", bufs=3)
+                us = []
+                for half in range(S // BANK):
+                    u = work.tile([P, BANK], F32, name="u", tag="u", bufs=4)
+                    nc.vector.tensor_tensor(u[:], b_ps[half][:], th[half][:], ALU.mult)
+                    us.append(u)
+                    if half == 0 and pending:
+                        gather(*pending.pop())
+                for half in range(S // BANK):
+                    nc.vector.tensor_tensor(h[:, BANK * half : BANK * (half + 1)], a_ps[half][:], us[half][:], ALU.max)
+                pending.append((b, i, h, ws))
+
+                step = PACK * b + i
+                if step == 0:
+                    w1_q.append(quantize(flat4(round_weight(w1_raw1, 1.0)), "w1_1"))
+                if step == 1:
+                    for a in range(H // BLK):
+                        raw4 = keep.tile([P, N], I32, name="w4_raw%d" % a, align_bytes=64)
+                        nc.sync.dma_start(out=raw4[:], in_=w4_words[a].rearrange("p n i -> p (n i)").bitcast(I32))
+                        w4_raw.append(raw4)
+                    load_scale_rows(nc.sync, w4_s_raw, 0, w4_scales)
+                    nc.sync.dma_start(list3[:], offs3)
+                    wgo_t = keep.tile([P, M], F32, name="wgo_t")
+                    nc.sync.dma_start(out=wgo_t[:], in_=wgo)
+                    gain_t = keep.tile([P, N // BLK, PACK], F32, name="gain_t")
+                    nc.sync.dma_start(out=gain_t[:], in_=gain.rearrange("(b p i) -> p b i", p=P, i=PACK))
+                if step in (2, 3):
+                    w3_q[step - 2, 0] = quantize(flat4(round_weight(load_weight(w3, step - 2, 0), -1.0)), "w3_%d0" % (step - 2))
+                if step == 4:
+                    x_q.append(quantize(round_x(0, [(nc.scalar.copy, slice(0, 64)), (nc.scalar.copy, slice(64, 128))])[:].rearrange("p m i -> p (m i)"), "x0"))
+                if step in (5, 6):
+                    w3_grouped[step - 5] = round_weight(load_weight(w3, step - 5, 1), -1.0)
+        gather(*pending.pop())
+        xb1 = round_x(1, [(nc.scalar.copy, slice(0, 96)), (nc.vector.tensor_copy, slice(96, 128))])
+        w4_w = {}
+
+        def deal_w4(c):
+            for a in range(H // BLK):
+                ww = keep.tile([P, BLK], I32, name="w4_w%d%d" % (a, c), align_bytes=64)
+                deal(ww[:], w4_raw[a][:, BLK * c : BLK * (c + 1)])
+                w4_w[a, c] = ww
+
+        w4_s = keep.tile([P, N], U8, name="w4_s", align_bytes=64)
+        deal(w4_s[:], w4_s_raw[:])
+        deal_w4(0)
+        x_q.append(quantize(xb1[:].rearrange("p m i -> p (m i)"), "x1"))
+        deal_w4(1)
+        for a in range(H // BLK):
+            w3_q[a, 1] = quantize(flat4(w3_grouped[a]), "w3_%d1" % a)
+
+        out_rows = out.rearrange("(c p i) t -> c i p t", p=P, i=PACK)
+        for c in range(N // BLK):
+            for i in range(PACK):
+                step = PACK * c + i
+                cols = slice(P * i, P * (i + 1))
+                w4_cols = slice(BLK * c + P * i, BLK * c + P * (i + 1))
+                tag = "pb" if step % 2 == 0 else "pa"
+                acc = psum.tile([P, BANK], F32, name="acc", tag=tag)
+                for a in range(H // BLK):
+                    nc.tensor.matmul_mx(
+                        out=acc[:], lhsT=w3_q[a, c][0][:, cols].bitcast(FP8X4), lhsT_scale=w3_q[a, c][1][:, cols],
+                        rhs=x_q[a][0][:].bitcast(FP8X4), rhs_scale=x_q[a][1][:], start=(a == 0), stop=False,
+                    )
+                    nc.tensor.matmul_mx(
+                        out=acc[:], lhsT=w4_w[a, c][:, cols].bitcast(FP8X4), lhsT_scale=w4_s[4 * a : P, w4_cols],
+                        rhs=x_q[a][0][:].bitcast(FP8X4), rhs_scale=x_q[a][1][:], start=False, stop=(a == H // BLK - 1),
+                    )
+                wg = scaled_rows(wgo_t, gain_t[:, c, i : i + 1], "wg")
+                sq = work.tile([P, M], F32, name="sq", tag="sq", bufs=3)
+                nc.scalar.activation(out=sq[:], in_=acc[:], func=ACT.Square)
+                page = pages[step % PAGES]
+                nc.vector.tensor_tensor(page[:].indirect(list3[:]), sq[:], wg[:], ALU.mult)
+                nc.sync.dma_start(out=out_rows[c, i], in_=page[:])

@@ -1,3 +1,4 @@
+import functools
 from contextlib import ExitStack
 
 import concourse.mybir as mybir
@@ -21,6 +22,7 @@ PACK = 4
 BLK = P * PACK
 BANK = 512
 PAGES = 4
+QUARTERS = [slice(32 * q, 32 * q + 32) for q in range(4)]
 
 
 def tile_list_sapline_leak_ledger_kernel(
@@ -53,17 +55,22 @@ def tile_list_sapline_leak_ledger_kernel(
             )
             return raw
 
-        def round_weight(raw, sign):
-            grouped = work.tile([P, PACK, P, PACK], BF16, name="grouped", tag="grouped", align_bytes=64)
-            for half in range(2):
-                ms = slice(64 * half, 64 * half + 64)
+        def round_weight(raw, sign, tag="grouped", bufs=2):
+            grouped = work.tile([P, PACK, P, PACK], BF16, name="grouped", tag=tag, bufs=bufs, align_bytes=64)
+
+            def part(ms):
                 nc.scalar.activation(
                     out=grouped[:].rearrange("p t m j -> p m j t")[:, ms],
                     in_=raw[:].rearrange("p j (m t) -> p m j t", t=PACK)[:, ms],
                     func=ACT.Copy,
                     scale=sign,
                 )
-            return grouped
+
+            return grouped, [functools.partial(part, ms) for ms in QUARTERS]
+
+        def run(jobs):
+            for job in jobs:
+                job()
 
         def quantize(grouped, name):
             codes = keep.tile([P, BLK], U32, name=name + "_codes", align_bytes=64)
@@ -74,20 +81,29 @@ def tile_list_sapline_leak_ledger_kernel(
         def flat4(grouped):
             return grouped[:].rearrange("p t m j -> p (t m j)")
 
-        def scaled_rows(rows, col, tag):
-            t = work.tile([P, M], F32, name=tag, tag=tag, bufs=4)
-            nc.scalar.activation(out=t[:], in_=rows[:], func=ACT.Copy, scale=col)
+        def scaled_rows(rows, col, on_gpsimd):
+            t = work.tile([P, M], F32, name="factor", tag="factor")
+            if on_gpsimd:
+                nc.gpsimd.tensor_scalar(t[:], rows[:], col, 0.0, ALU.mult, ALU.add)
+            else:
+                nc.scalar.activation(out=t[:], in_=rows[:], func=ACT.Copy, scale=col)
             return t
 
         list1 = keep.tile([P, S // 16], U16, name="list1")
         list2 = keep.tile([P, M // 16], U16, name="list2")
         list3 = keep.tile([P, M // 16], U16, name="list3")
         tab_s = keep.tile([P, T], U8, name="tab_s", align_bytes=64)
-        w2_s_raw = keep.tile([P, H], U8, name="w2_s_raw", align_bytes=64)
-        w4_s_raw = keep.tile([P, N], U8, name="w4_s_raw", align_bytes=64)
+        w2_s_raw = keep.tile([P, BLK], U8, name="w2_s_raw", align_bytes=64)
+        late_s_raw = keep.tile([P, N], U8, name="late_s_raw", align_bytes=64)
+        v_s = keep.tile([P, S], U8, name="v_s", align_bytes=64)
         nc.vector.memset(tab_s[:].bitcast(I32), 0)
+        pages = []
+        for k in range(PAGES):
+            page = keep.tile([P, T2], F32, name="page%d" % k)
+            nc.vector.memset(page[:], 0.0)
+            pages.append(page)
         nc.vector.memset(w2_s_raw[:].bitcast(I32), 0)
-        nc.vector.memset(w4_s_raw[:].bitcast(I32), 0)
+        nc.vector.memset(late_s_raw[:].bitcast(I32), 0)
 
         nc.sync.dma_start(list1[:], offs)
         w1_raw0 = load_weight(w1, 0, 0)
@@ -96,134 +112,168 @@ def tile_list_sapline_leak_ledger_kernel(
         nc.sync.dma_start(out=w2_raw[:].bitcast(I32), in_=w2_words[0].bitcast(I32))
         tab_w = keep.tile([P, T], I32, name="tab_w", align_bytes=64)
         nc.sync.dma_start(out=tab_w[:], in_=tab_words[0].rearrange("p t i -> p (t i)").bitcast(I32))
-        load_scale_rows(nc.sync, w2_s_raw, 0, w2_scales)
+        load_scale_rows(nc.scalar, w2_s_raw, 0, w2_scales[:, :, 0:BLK])
         nc.sync.dma_start(list2[:], offs2)
         wgt_t = keep.tile([P, M], F32, name="wgt_t")
         nc.sync.dma_start(out=wgt_t[:], in_=wgt)
         sens_t = keep.tile([P, H // BLK, PACK], F32, name="sens_t")
         nc.sync.dma_start(out=sens_t[:], in_=sens.rearrange("(b p i) -> p b i", p=P, i=PACK))
         w1_raw1 = load_weight(w1, 0, 1)
+        load_scale_rows(nc.sync, late_s_raw[:, 0:BLK], 0, w2_scales[:, :, BLK : 2 * BLK])
+        load_scale_rows(nc.sync, late_s_raw, 4, w4_scales)
 
-        v_s = keep.tile([P, S], U8, name="v_s", align_bytes=64)
         nc.vector.tensor_copy(v_s[:], tab_s[:].indirect(list1[:]))
         w2_w = keep.tile([P, 2 * H], U8, name="w2_w", align_bytes=64)
-        w2_s = keep.tile([P, H], U8, name="w2_s", align_bytes=64)
+        w2_s0 = keep.tile([P, BLK], U8, name="w2_s0", align_bytes=64)
+        late_s = keep.tile([P, N], U8, name="late_s", align_bytes=64)
+        w2_s = [w2_s0, late_s]
         deal(w2_w[:].bitcast(U16), w2_raw[:].bitcast(U16))
-        w1_q = [quantize(flat4(round_weight(w1_raw0, 1.0)), "w1_0")]
+        grouped, jobs = round_weight(w1_raw0, 1.0)
+        run(jobs)
+        w1_q = [quantize(flat4(grouped), "w1_0")]
+        deal(w2_s0[:], w2_s_raw[:])
         v_w = []
         for half in range(S // BANK):
             vw = keep.tile([P, BANK], U32, name="v_w%d" % half, align_bytes=64)
             nc.vector.tensor_copy(vw[:], tab_w[:].bitcast(U32).indirect(list1[:, 32 * half : 32 * half + 32]))
             v_w.append(vw)
-            if half == 0:
-                deal(w2_s[:], w2_s_raw[:])
-        pages = []
-        for k in range(PAGES):
-            page = keep.tile([P, T2], F32, name="page%d" % k)
-            nc.vector.memset(page[:], 0.0)
-            pages.append(page)
 
         w3_q = {}
-        w3_grouped = {}
-        w4_raw = []
         x_q = []
-        picked = {}
-        pending = []
+        picked = []
+        steps = H // P
 
-        def gather(b, i, h, ws):
+        w4_raw = []
+        for a in range(H // BLK):
+            raw4 = keep.tile([P, N], I32, name="w4_raw%d" % a, align_bytes=64)
+            w4_raw.append(raw4)
+        wgo_t = keep.tile([P, M], F32, name="wgo_t")
+        gain_t = keep.tile([P, N // BLK, PACK], F32, name="gain_t")
+
+        def front(step):
+            b, i = divmod(step, PACK)
+            cols = slice(P * i, P * (i + 1))
+            w2_bytes = slice(2 * P * step, 2 * P * (step + 1))
+            a_ps, b_ps, th = [], [], []
+            h = work.tile([P, S], F32, name="h", tag="h")
+            for half in range(S // BANK):
+                js = slice(BANK * half, BANK * (half + 1))
+                pa = psum.tile([P, BANK], F32, name="pa", tag="pa")
+                pb = psum.tile([P, BANK], F32, name="pb", tag="pb")
+                nc.tensor.matmul_mx(
+                    out=pa[:], lhsT=w1_q[b][0][:, cols].bitcast(FP8X4), lhsT_scale=w1_q[b][1][:, cols],
+                    rhs=v_w[half][:].bitcast(FP8X4), rhs_scale=v_s[:, js], start=True, stop=True,
+                )
+                nc.tensor.matmul_mx(
+                    out=pb[:], lhsT=w2_w[:, w2_bytes].bitcast(FP4X4), lhsT_scale=w2_s[b][:, cols],
+                    rhs=v_w[half][:].bitcast(FP8X4), rhs_scale=v_s[:, js], start=True, stop=True,
+                )
+                t = work.tile([P, BANK], F32, name="tanh_a", tag="tanh_a", bufs=4)
+                nc.scalar.activation(out=t[:], in_=pa[:], func=ACT.Tanh)
+                if half == 0 and step > 0:
+                    b_sb = work.tile([P, BANK], F32, name="b_sb", tag="b_sb")
+                    nc.scalar.copy(out=b_sb[:], in_=pb[:])
+                    nc.gpsimd.tensor_tensor(h[:, js], b_sb[:], t[:], ALU.mult)
+                a_ps.append(pa)
+                b_ps.append(pb)
+                th.append(t)
+            ws = scaled_rows(wgt_t, sens_t[:, b, i : i + 1], step > 1)
+            return a_ps, b_ps, th, h, ws
+
+        def gather(step, h, ws):
+            b, i = divmod(step, PACK)
             if i == 0:
-                picked[b] = work.tile([P, PACK, M], F32, name="picked", tag="picked")
+                picked.append(work.tile([P, PACK, M], F32, name="picked", tag="picked%d" % b, bufs=1, align_bytes=64))
             nc.vector.tensor_tensor(picked[b][:, i, :], h[:].indirect(list2[:]), ws[:], ALU.mult)
 
-        def round_x(b, parts):
-            xb = work.tile([P, M, PACK], BF16, name="xb", tag="xb", align_bytes=64)
-            for copy, cs in parts:
+        def round_x(b):
+            xb = work.tile([P, M, PACK], BF16, name="xb", tag="xb", bufs=1, align_bytes=64)
+
+            def part(copy, cs):
                 copy(
                     out=xb[:].rearrange("p (c e) i -> p c i e", e=4)[:, cs],
                     in_=picked[b][:].rearrange("p i (c e) -> p c i e", e=4)[:, cs],
                 )
-            return xb
 
-        for b in range(H // BLK):
-            for i in range(PACK):
-                cols = slice(P * i, P * (i + 1))
-                w2_cols = slice(BLK * b + P * i, BLK * b + P * (i + 1))
-                w2_bytes = slice(2 * (BLK * b + P * i), 2 * (BLK * b + P * (i + 1)))
-                a_ps, b_ps, th = [], [], []
-                for half in range(S // BANK):
-                    js = slice(BANK * half, BANK * (half + 1))
-                    pa = psum.tile([P, BANK], F32, name="pa", tag="pa")
-                    pb = psum.tile([P, BANK], F32, name="pb", tag="pb")
-                    nc.tensor.matmul_mx(
-                        out=pa[:], lhsT=w1_q[b][0][:, cols].bitcast(FP8X4), lhsT_scale=w1_q[b][1][:, cols],
-                        rhs=v_w[half][:].bitcast(FP8X4), rhs_scale=v_s[:, js], start=True, stop=True,
-                    )
-                    nc.tensor.matmul_mx(
-                        out=pb[:], lhsT=w2_w[:, w2_bytes].bitcast(FP4X4), lhsT_scale=w2_s[:, w2_cols],
-                        rhs=v_w[half][:].bitcast(FP8X4), rhs_scale=v_s[:, js], start=True, stop=True,
-                    )
-                    t = work.tile([P, BANK], F32, name="tanh_a", tag="tanh_a", bufs=4)
-                    nc.scalar.activation(out=t[:], in_=pa[:], func=ACT.Tanh)
-                    a_ps.append(pa)
-                    b_ps.append(pb)
-                    th.append(t)
-                ws = scaled_rows(wgt_t, sens_t[:, b, i : i + 1], "ws")
-                h = work.tile([P, S], F32, name="h", tag="h", bufs=3)
-                us = []
-                for half in range(S // BANK):
-                    u = work.tile([P, BANK], F32, name="u", tag="u", bufs=4)
-                    nc.vector.tensor_tensor(u[:], b_ps[half][:], th[half][:], ALU.mult)
-                    us.append(u)
-                    if half == 0 and pending:
-                        gather(*pending.pop())
-                for half in range(S // BANK):
-                    nc.vector.tensor_tensor(h[:, BANK * half : BANK * (half + 1)], a_ps[half][:], us[half][:], ALU.max)
-                pending.append((b, i, h, ws))
+            return xb, part
 
-                step = PACK * b + i
-                if step == 0:
-                    w1_q.append(quantize(flat4(round_weight(w1_raw1, 1.0)), "w1_1"))
-                if step == 1:
-                    for a in range(H // BLK):
-                        raw4 = keep.tile([P, N], I32, name="w4_raw%d" % a, align_bytes=64)
-                        nc.sync.dma_start(out=raw4[:], in_=w4_words[a].rearrange("p n i -> p (n i)").bitcast(I32))
-                        w4_raw.append(raw4)
-                    load_scale_rows(nc.sync, w4_s_raw, 0, w4_scales)
-                    nc.sync.dma_start(list3[:], offs3)
-                    wgo_t = keep.tile([P, M], F32, name="wgo_t")
-                    nc.sync.dma_start(out=wgo_t[:], in_=wgo)
-                    gain_t = keep.tile([P, N // BLK, PACK], F32, name="gain_t")
-                    nc.sync.dma_start(out=gain_t[:], in_=gain.rearrange("(b p i) -> p b i", p=P, i=PACK))
-                if step in (2, 3):
-                    w3_q[step - 2, 0] = quantize(flat4(round_weight(load_weight(w3, step - 2, 0), -1.0)), "w3_%d0" % (step - 2))
-                if step == 4:
-                    x_q.append(quantize(round_x(0, [(nc.scalar.copy, slice(0, 64)), (nc.scalar.copy, slice(64, 128))])[:].rearrange("p m i -> p (m i)"), "x0"))
-                if step in (5, 6):
-                    w3_grouped[step - 5] = round_weight(load_weight(w3, step - 5, 1), -1.0)
-        gather(*pending.pop())
-        xb1 = round_x(1, [(nc.scalar.copy, slice(0, 96)), (nc.vector.tensor_copy, slice(96, 128))])
-        w4_w = {}
+        def flat3(xb):
+            return xb[:].rearrange("p m i -> p (m i)")
 
-        def deal_w4(c):
+        tiles = {0: front(0)}
+        for step in range(steps):
+            a_ps, b_ps, th, h, ws = tiles[step]
+            lo, hi = h[:, 0:BANK], h[:, BANK:S]
+            if step == 0:
+                nc.vector.tensor_tensor(lo, b_ps[0][:], th[0][:], ALU.mult)
+                nc.vector.tensor_tensor(lo, a_ps[0][:], lo, ALU.max)
+            nc.vector.tensor_tensor(hi, b_ps[1][:], th[1][:], ALU.mult)
+            if step > 0:
+                gather(step - 1, *tiles[step - 1][3:])
+            if step == 1:
+                deal(late_s[:, 0:BLK], late_s_raw[:, 0:BLK])
+            if step == 2:
+                w1_q.append(quantize(flat4(g_w1), "w1_1"))
+            if step == 4:
+                w3_q[0, 0] = quantize(flat4(g_00), "w3_00")
+            if step == 5:
+                w3_q[1, 0] = quantize(flat4(g_10), "w3_10")
+            if step == 6:
+                x_q.append(quantize(flat3(xb0), "x0"))
+            if step + 1 < steps:
+                tiles[step + 1] = front(step + 1)
+            if step > 0:
+                nc.vector.tensor_tensor(lo, a_ps[0][:], lo, ALU.max)
+            nc.vector.tensor_tensor(hi, a_ps[1][:], hi, ALU.max)
+
+            if step == 0:
+                g_w1, jobs = round_weight(w1_raw1, 1.0)
+                run(jobs[:2])
+                g_00, jobs00 = round_weight(load_weight(w3, 0, 0), -1.0)
+                for a in range(H // BLK):
+                    nc.sync.dma_start(out=w4_raw[a][:], in_=w4_words[a].rearrange("p n i -> p (n i)").bitcast(I32))
+                nc.sync.dma_start(list3[:], offs3)
+                nc.sync.dma_start(out=wgo_t[:], in_=wgo)
+                nc.sync.dma_start(out=gain_t[:], in_=gain.rearrange("(b p i) -> p b i", p=P, i=PACK))
+            if step == 1:
+                run(jobs[2:] + jobs00[:1])
+            if step == 2:
+                run(jobs00[1:])
+                g_10, jobs10 = round_weight(load_weight(w3, 1, 0), -1.0)
+            if step == 3:
+                run(jobs10[:3])
+            if step == 4:
+                run(jobs10[3:])
+                xb0, part = round_x(0)
+                run([functools.partial(part, nc.scalar.copy, cs) for cs in QUARTERS[:2]])
+            if step == 5:
+                run([functools.partial(part, nc.scalar.copy, cs) for cs in QUARTERS[2:]])
+                g_01, jobs01 = round_weight(load_weight(w3, 0, 1), -1.0, "picked0", 1)
+            if step == 6:
+                run(jobs01)
+        gather(steps - 1, *tiles[steps - 1][3:])
+        xb1, part = round_x(1)
+        part(nc.scalar.copy, slice(0, 56))
+        part(nc.vector.tensor_copy, slice(56, 128))
+        w4_w = []
+
+        def deal_w4(c, tag):
+            ww = work.tile([P, H // BLK, BLK], I32, name="w4_w", tag=tag, bufs=1, align_bytes=64)
             for a in range(H // BLK):
-                ww = keep.tile([P, BLK], I32, name="w4_w%d%d" % (a, c), align_bytes=64)
-                deal(ww[:], w4_raw[a][:, BLK * c : BLK * (c + 1)])
-                w4_w[a, c] = ww
+                deal(ww[:, a, :], w4_raw[a][:, BLK * c : BLK * (c + 1)])
+            w4_w.append(ww)
 
-        w4_s = keep.tile([P, N], U8, name="w4_s", align_bytes=64)
-        deal(w4_s[:], w4_s_raw[:])
-        deal_w4(0)
+        deal_w4(0, "w4_w")
         x_q.append(quantize(xb1[:].rearrange("p m i -> p (m i)"), "x1"))
-        deal_w4(1)
-        for a in range(H // BLK):
-            w3_q[a, 1] = quantize(flat4(w3_grouped[a]), "w3_%d1" % a)
+        deal_w4(1, "xb")
+        deal(late_s[:, BLK:N], late_s_raw[:, BLK:N])
+        w3_q[0, 1] = quantize(flat4(g_01), "w3_01")
 
         out_rows = out.rearrange("(c p i) t -> c i p t", p=P, i=PACK)
         for c in range(N // BLK):
             for i in range(PACK):
                 step = PACK * c + i
                 cols = slice(P * i, P * (i + 1))
-                w4_cols = slice(BLK * c + P * i, BLK * c + P * (i + 1))
                 tag = "pb" if step % 2 == 0 else "pa"
                 acc = psum.tile([P, BANK], F32, name="acc", tag=tag)
                 for a in range(H // BLK):
@@ -232,12 +282,16 @@ def tile_list_sapline_leak_ledger_kernel(
                         rhs=x_q[a][0][:].bitcast(FP8X4), rhs_scale=x_q[a][1][:], start=(a == 0), stop=False,
                     )
                     nc.tensor.matmul_mx(
-                        out=acc[:], lhsT=w4_w[a, c][:, cols].bitcast(FP8X4), lhsT_scale=w4_s[4 * a : P, w4_cols],
+                        out=acc[:], lhsT=w4_w[c][:, a, cols].bitcast(FP8X4), lhsT_scale=late_s[4 + 4 * a : P, BLK * c + P * i : BLK * c + P * (i + 1)],
                         rhs=x_q[a][0][:].bitcast(FP8X4), rhs_scale=x_q[a][1][:], start=False, stop=(a == H // BLK - 1),
                     )
-                wg = scaled_rows(wgo_t, gain_t[:, c, i : i + 1], "wg")
+                wg = scaled_rows(wgo_t, gain_t[:, c, i : i + 1], False)
                 sq = work.tile([P, M], F32, name="sq", tag="sq", bufs=3)
                 nc.scalar.activation(out=sq[:], in_=acc[:], func=ACT.Square)
                 page = pages[step % PAGES]
                 nc.vector.tensor_tensor(page[:].indirect(list3[:]), sq[:], wg[:], ALU.mult)
                 nc.sync.dma_start(out=out_rows[c, i], in_=page[:])
+                if step == 0:
+                    g_11, jobs = round_weight(load_weight(w3, 1, 1), -1.0, "picked1", 1)
+                    run(jobs)
+                    w3_q[1, 1] = quantize(flat4(g_11), "w3_11")

@@ -22,6 +22,7 @@ PACK = 4
 BLK = P * PACK
 BANK = 512
 PAGES = 4
+HALVES = [slice(0, 64), slice(64, 128)]
 QUARTERS = [slice(32 * q, 32 * q + 32) for q in range(4)]
 
 
@@ -55,7 +56,7 @@ def tile_list_sapline_leak_ledger_kernel(
             )
             return raw
 
-        def round_weight(raw, sign, tag="grouped", bufs=2):
+        def round_weight(raw, sign, parts, tag="grouped", bufs=2):
             grouped = work.tile([P, PACK, P, PACK], BF16, name="grouped", tag=tag, bufs=bufs, align_bytes=64)
 
             def part(ms):
@@ -66,7 +67,7 @@ def tile_list_sapline_leak_ledger_kernel(
                     scale=sign,
                 )
 
-            return grouped, [functools.partial(part, ms) for ms in QUARTERS]
+            return grouped, [functools.partial(part, ms) for ms in parts]
 
         def run(jobs):
             for job in jobs:
@@ -81,12 +82,9 @@ def tile_list_sapline_leak_ledger_kernel(
         def flat4(grouped):
             return grouped[:].rearrange("p t m j -> p (t m j)")
 
-        def scaled_rows(rows, col, on_gpsimd):
-            t = work.tile([P, M], F32, name="factor", tag="factor")
-            if on_gpsimd:
-                nc.gpsimd.tensor_scalar(t[:], rows[:], col, 0.0, ALU.mult, ALU.add)
-            else:
-                nc.scalar.activation(out=t[:], in_=rows[:], func=ACT.Copy, scale=col)
+        def scaled_rows(rows, col, tag, bufs):
+            t = work.tile([P, M], F32, name="factor", tag=tag, bufs=bufs)
+            nc.scalar.activation(out=t[:], in_=rows[:], func=ACT.Copy, scale=col)
             return t
 
         list1 = keep.tile([P, S // 16], U16, name="list1")
@@ -115,9 +113,9 @@ def tile_list_sapline_leak_ledger_kernel(
         load_scale_rows(nc.scalar, w2_s_raw, 0, w2_scales[:, :, 0:BLK])
         nc.sync.dma_start(list2[:], offs2)
         wgt_t = keep.tile([P, M], F32, name="wgt_t")
-        nc.sync.dma_start(out=wgt_t[:], in_=wgt)
+        nc.scalar.dma_start(out=wgt_t[:], in_=wgt)
         sens_t = keep.tile([P, H // BLK, PACK], F32, name="sens_t")
-        nc.sync.dma_start(out=sens_t[:], in_=sens.rearrange("(b p i) -> p b i", p=P, i=PACK))
+        nc.scalar.dma_start(out=sens_t[:], in_=sens.rearrange("(b p i) -> p b i", p=P, i=PACK))
         w1_raw1 = load_weight(w1, 0, 1)
         load_scale_rows(nc.sync, late_s_raw[:, 0:BLK], 0, w2_scales[:, :, BLK : 2 * BLK])
         load_scale_rows(nc.sync, late_s_raw, 4, w4_scales)
@@ -128,7 +126,7 @@ def tile_list_sapline_leak_ledger_kernel(
         late_s = keep.tile([P, N], U8, name="late_s", align_bytes=64)
         w2_s = [w2_s0, late_s]
         deal(w2_w[:].bitcast(U16), w2_raw[:].bitcast(U16))
-        grouped, jobs = round_weight(w1_raw0, 1.0)
+        grouped, jobs = round_weight(w1_raw0, 1.0, HALVES)
         run(jobs)
         w1_q = [quantize(flat4(grouped), "w1_0")]
         deal(w2_s0[:], w2_s_raw[:])
@@ -177,8 +175,7 @@ def tile_list_sapline_leak_ledger_kernel(
                 a_ps.append(pa)
                 b_ps.append(pb)
                 th.append(t)
-            ws = scaled_rows(wgt_t, sens_t[:, b, i : i + 1], step > 1)
-            return a_ps, b_ps, th, h, ws
+            return a_ps, b_ps, th, h, ws_all[step]
 
         def gather(step, h, ws):
             b, i = divmod(step, PACK)
@@ -200,6 +197,7 @@ def tile_list_sapline_leak_ledger_kernel(
         def flat3(xb):
             return xb[:].rearrange("p m i -> p (m i)")
 
+        ws_all = [scaled_rows(wgt_t, sens_t[:, s // PACK, s % PACK : s % PACK + 1], "ws", steps) for s in range(steps)]
         tiles = {0: front(0)}
         for step in range(steps):
             a_ps, b_ps, th, h, ws = tiles[step]
@@ -216,9 +214,9 @@ def tile_list_sapline_leak_ledger_kernel(
                 w1_q.append(quantize(flat4(g_w1), "w1_1"))
             if step == 4:
                 w3_q[0, 0] = quantize(flat4(g_00), "w3_00")
-            if step == 5:
-                w3_q[1, 0] = quantize(flat4(g_10), "w3_10")
             if step == 6:
+                w3_q[1, 0] = quantize(flat4(g_10), "w3_10")
+            if step == 7:
                 x_q.append(quantize(flat3(xb0), "x0"))
             if step + 1 < steps:
                 tiles[step + 1] = front(step + 1)
@@ -227,29 +225,27 @@ def tile_list_sapline_leak_ledger_kernel(
             nc.vector.tensor_tensor(hi, a_ps[1][:], hi, ALU.max)
 
             if step == 0:
-                g_w1, jobs = round_weight(w1_raw1, 1.0)
-                run(jobs[:2])
-                g_00, jobs00 = round_weight(load_weight(w3, 0, 0), -1.0)
+                g_w1, jobs = round_weight(w1_raw1, 1.0, HALVES)
+                jobs[0]()
+                g_00, jobs00 = round_weight(load_weight(w3, 0, 0), -1.0, HALVES)
                 for a in range(H // BLK):
                     nc.sync.dma_start(out=w4_raw[a][:], in_=w4_words[a].rearrange("p n i -> p (n i)").bitcast(I32))
                 nc.sync.dma_start(list3[:], offs3)
                 nc.sync.dma_start(out=wgo_t[:], in_=wgo)
                 nc.sync.dma_start(out=gain_t[:], in_=gain.rearrange("(b p i) -> p b i", p=P, i=PACK))
             if step == 1:
-                run(jobs[2:] + jobs00[:1])
-            if step == 2:
-                run(jobs00[1:])
-                g_10, jobs10 = round_weight(load_weight(w3, 1, 0), -1.0)
-            if step == 3:
-                run(jobs10[:3])
+                jobs[1]()
+            if step in (2, 3):
+                jobs00[step - 2]()
             if step == 4:
-                run(jobs10[3:])
-                xb0, part = round_x(0)
-                run([functools.partial(part, nc.scalar.copy, cs) for cs in QUARTERS[:2]])
+                g_10, jobs10 = round_weight(load_weight(w3, 1, 0), -1.0, HALVES)
+                run(jobs10)
             if step == 5:
-                run([functools.partial(part, nc.scalar.copy, cs) for cs in QUARTERS[2:]])
-                g_01, jobs01 = round_weight(load_weight(w3, 0, 1), -1.0, "picked0", 1)
+                xb0, part = round_x(0)
+            if step in (5, 6):
+                part(nc.scalar.copy, HALVES[step - 5])
             if step == 6:
+                g_01, jobs01 = round_weight(load_weight(w3, 0, 1), -1.0, HALVES, "picked0", 1)
                 run(jobs01)
         gather(steps - 1, *tiles[steps - 1][3:])
         xb1, part = round_x(1)
@@ -285,13 +281,13 @@ def tile_list_sapline_leak_ledger_kernel(
                         out=acc[:], lhsT=w4_w[c][:, a, cols].bitcast(FP8X4), lhsT_scale=late_s[4 + 4 * a : P, BLK * c + P * i : BLK * c + P * (i + 1)],
                         rhs=x_q[a][0][:].bitcast(FP8X4), rhs_scale=x_q[a][1][:], start=False, stop=(a == H // BLK - 1),
                     )
-                wg = scaled_rows(wgo_t, gain_t[:, c, i : i + 1], False)
+                wg = scaled_rows(wgo_t, gain_t[:, c, i : i + 1], "b_sb", 2)
                 sq = work.tile([P, M], F32, name="sq", tag="sq", bufs=3)
                 nc.scalar.activation(out=sq[:], in_=acc[:], func=ACT.Square)
                 page = pages[step % PAGES]
                 nc.vector.tensor_tensor(page[:].indirect(list3[:]), sq[:], wg[:], ALU.mult)
                 nc.sync.dma_start(out=out_rows[c, i], in_=page[:])
                 if step == 0:
-                    g_11, jobs = round_weight(load_weight(w3, 1, 1), -1.0, "picked1", 1)
+                    grouped, jobs = round_weight(load_weight(w3, 1, 1), -1.0, QUARTERS, "picked1", 1)
                     run(jobs)
-                    w3_q[1, 1] = quantize(flat4(g_11), "w3_11")
+                    w3_q[1, 1] = quantize(flat4(grouped), "w3_11")

@@ -50,7 +50,7 @@ def tile_list_sapline_leak_ledger_kernel(
             )
 
         def load_weight(w, a, c):
-            raw = work.tile([P, PACK, BLK], F32, name="raw", tag="raw")
+            raw = work.tile([P, PACK, BLK], F32, name="raw", tag="raw", bufs=3)
             nc.sync.dma_start(
                 out=raw[:], in_=w[BLK * a : BLK * (a + 1), BLK * c : BLK * (c + 1)].rearrange("(p j) n -> p j n", j=PACK)
             )
@@ -153,7 +153,7 @@ def tile_list_sapline_leak_ledger_kernel(
             cols = slice(P * i, P * (i + 1))
             w2_bytes = slice(2 * P * step, 2 * P * (step + 1))
             a_ps, b_ps, th = [], [], []
-            h = work.tile([P, S], F32, name="h", tag="h")
+            h = work.tile([P, S], F32, name="h", tag="h", align_bytes=64)
             for half in range(S // BANK):
                 js = slice(BANK * half, BANK * (half + 1))
                 pa = psum.tile([P, BANK], F32, name="pa", tag="pa")
@@ -197,6 +197,14 @@ def tile_list_sapline_leak_ledger_kernel(
         def flat3(xb):
             return xb[:].rearrange("p m i -> p (m i)")
 
+        w4_w = []
+
+        def deal_w4(c, tag):
+            ww = work.tile([P, H // BLK, BLK], I32, name="w4_w", tag=tag, bufs=1, align_bytes=64)
+            for a in range(H // BLK):
+                deal(ww[:, a, :], w4_raw[a][:, BLK * c : BLK * (c + 1)])
+            w4_w.append(ww)
+
         ws_all = [scaled_rows(wgt_t, sens_t[:, s // PACK, s % PACK : s % PACK + 1], "ws", steps) for s in range(steps)]
         tiles = {0: front(0)}
         for step in range(steps):
@@ -214,10 +222,12 @@ def tile_list_sapline_leak_ledger_kernel(
                 w1_q.append(quantize(flat4(g_w1), "w1_1"))
             if step == 4:
                 w3_q[0, 0] = quantize(flat4(g_00), "w3_00")
-            if step == 6:
+            if step == 5:
                 w3_q[1, 0] = quantize(flat4(g_10), "w3_10")
-            if step == 7:
+            if step == 6:
                 x_q.append(quantize(flat3(xb0), "x0"))
+            if step == 7:
+                deal_w4(0, "w4_w")
             if step + 1 < steps:
                 tiles[step + 1] = front(step + 1)
             if step > 0:
@@ -225,42 +235,36 @@ def tile_list_sapline_leak_ledger_kernel(
             nc.vector.tensor_tensor(hi, a_ps[1][:], hi, ALU.max)
 
             if step == 0:
-                g_w1, jobs = round_weight(w1_raw1, 1.0, HALVES)
-                jobs[0]()
-                g_00, jobs00 = round_weight(load_weight(w3, 0, 0), -1.0, HALVES)
+                g_w1, jobs = round_weight(w1_raw1, 1.0, QUARTERS)
+                g_00, more = round_weight(load_weight(w3, 0, 0), -1.0, QUARTERS)
+                jobs = jobs + more
                 for a in range(H // BLK):
                     nc.sync.dma_start(out=w4_raw[a][:], in_=w4_words[a].rearrange("p n i -> p (n i)").bitcast(I32))
                 nc.sync.dma_start(list3[:], offs3)
                 nc.sync.dma_start(out=wgo_t[:], in_=wgo)
                 nc.sync.dma_start(out=gain_t[:], in_=gain.rearrange("(b p i) -> p b i", p=P, i=PACK))
-            if step == 1:
-                jobs[1]()
-            if step in (2, 3):
-                jobs00[step - 2]()
+            if step == 2:
+                g_10, more = round_weight(load_weight(w3, 1, 0), -1.0, QUARTERS)
+                jobs = jobs + more
             if step == 4:
-                g_10, jobs10 = round_weight(load_weight(w3, 1, 0), -1.0, HALVES)
-                run(jobs10)
-            if step == 5:
                 xb0, part = round_x(0)
-            if step in (5, 6):
-                part(nc.scalar.copy, HALVES[step - 5])
-            if step == 6:
-                g_01, jobs01 = round_weight(load_weight(w3, 0, 1), -1.0, HALVES, "picked0", 1)
-                run(jobs01)
+                jobs = jobs + [functools.partial(part, nc.scalar.copy, cs) for cs in QUARTERS]
+            run(jobs[:3])
+            jobs = jobs[3:]
+        g_01, jobs = round_weight(load_weight(w3, 0, 1), -1.0, QUARTERS, "h", 2)
+        run(jobs)
         gather(steps - 1, *tiles[steps - 1][3:])
         xb1, part = round_x(1)
-        part(nc.scalar.copy, slice(0, 56))
-        part(nc.vector.tensor_copy, slice(56, 128))
-        w4_w = []
-
-        def deal_w4(c, tag):
-            ww = work.tile([P, H // BLK, BLK], I32, name="w4_w", tag=tag, bufs=1, align_bytes=64)
-            for a in range(H // BLK):
-                deal(ww[:, a, :], w4_raw[a][:, BLK * c : BLK * (c + 1)])
-            w4_w.append(ww)
-
-        deal_w4(0, "w4_w")
-        x_q.append(quantize(xb1[:].rearrange("p m i -> p (m i)"), "x1"))
+        part(nc.scalar.copy, HALVES[0])
+        part(nc.vector.tensor_copy, HALVES[1])
+        x1_codes = keep.tile([P, M], U32, name="x1_codes", align_bytes=64)
+        x1_scales = keep.tile([P, M], U8, name="x1_scales", align_bytes=64)
+        m_halves = [slice(M // 2, M), slice(0, M // 2)]
+        for ms in m_halves:
+            nc.vector.quantize_mx(
+                out=x1_codes[:, ms].bitcast(FP8X4), scales=x1_scales[:, ms], in_=xb1[:, ms, :].rearrange("p m i -> p (m i)")
+            )
+        x_q.append((x1_codes, x1_scales))
         deal_w4(1, "xb")
         deal(late_s[:, BLK:N], late_s_raw[:, BLK:N])
         w3_q[0, 1] = quantize(flat4(g_01), "w3_01")
@@ -270,24 +274,27 @@ def tile_list_sapline_leak_ledger_kernel(
             for i in range(PACK):
                 step = PACK * c + i
                 cols = slice(P * i, P * (i + 1))
-                tag = "pb" if step % 2 == 0 else "pa"
-                acc = psum.tile([P, BANK], F32, name="acc", tag=tag)
-                for a in range(H // BLK):
-                    nc.tensor.matmul_mx(
-                        out=acc[:], lhsT=w3_q[a, c][0][:, cols].bitcast(FP8X4), lhsT_scale=w3_q[a, c][1][:, cols],
-                        rhs=x_q[a][0][:].bitcast(FP8X4), rhs_scale=x_q[a][1][:], start=(a == 0), stop=False,
-                    )
-                    nc.tensor.matmul_mx(
-                        out=acc[:], lhsT=w4_w[c][:, a, cols].bitcast(FP8X4), lhsT_scale=late_s[4 + 4 * a : P, BLK * c + P * i : BLK * c + P * (i + 1)],
-                        rhs=x_q[a][0][:].bitcast(FP8X4), rhs_scale=x_q[a][1][:], start=False, stop=(a == H // BLK - 1),
-                    )
                 wg = scaled_rows(wgo_t, gain_t[:, c, i : i + 1], "b_sb", 2)
-                sq = work.tile([P, M], F32, name="sq", tag="sq", bufs=3)
-                nc.scalar.activation(out=sq[:], in_=acc[:], func=ACT.Square)
+                if step == 0:
+                    sq = work.tile([P, M], F32, name="sq", tag="first_sq", bufs=1, align_bytes=64)
+                else:
+                    sq = work.tile([P, M], F32, name="sq", tag="sq", bufs=3)
+                for k, ms in enumerate(m_halves if step == 0 else [slice(0, M)]):
+                    acc = psum.tile([P, ms.stop - ms.start], F32, name="acc", tag=("pb", "pa")[(step + k) % 2])
+                    for a in range(H // BLK):
+                        nc.tensor.matmul_mx(
+                            out=acc[:], lhsT=w3_q[a, c][0][:, cols].bitcast(FP8X4), lhsT_scale=w3_q[a, c][1][:, cols],
+                            rhs=x_q[a][0][:, ms].bitcast(FP8X4), rhs_scale=x_q[a][1][:, ms], start=(a == 0), stop=False,
+                        )
+                        nc.tensor.matmul_mx(
+                            out=acc[:], lhsT=w4_w[c][:, a, cols].bitcast(FP8X4), lhsT_scale=late_s[4 + 4 * a : P, BLK * c + P * i : BLK * c + P * (i + 1)],
+                            rhs=x_q[a][0][:, ms].bitcast(FP8X4), rhs_scale=x_q[a][1][:, ms], start=False, stop=(a == H // BLK - 1),
+                        )
+                    nc.scalar.activation(out=sq[:, ms], in_=acc[:], func=ACT.Square)
                 page = pages[step % PAGES]
                 nc.vector.tensor_tensor(page[:].indirect(list3[:]), sq[:], wg[:], ALU.mult)
                 nc.sync.dma_start(out=out_rows[c, i], in_=page[:])
                 if step == 0:
-                    grouped, jobs = round_weight(load_weight(w3, 1, 1), -1.0, QUARTERS, "picked1", 1)
+                    grouped, jobs = round_weight(load_weight(w3, 1, 1), -1.0, QUARTERS, "first_sq", 1)
                     run(jobs)
                     w3_q[1, 1] = quantize(flat4(grouped), "w3_11")

import functools
from contextlib import ExitStack

import concourse.mybir as mybir

K, H, N, T, S, M, T2 = 512, 1024, 1024, 4096, 1024, 512, 1024
FLOPS = 2 * (2 * K * H * S + 2 * H * N * M)

F32 = mybir.dt.float32
BF16 = mybir.dt.bfloat16
I32 = mybir.dt.int32
U32 = mybir.dt.uint32
U16 = mybir.dt.uint16
U8 = mybir.dt.uint8
FP8X4 = mybir.dt.float8_e4m3fn_x4
FP4X4 = mybir.dt.float4_e2m1fn_x4
ACT = mybir.ActivationFunctionType
ALU = mybir.AluOpType

P = 128
PACK = 4
BLK = P * PACK
BANK = 512
PAGES = 4
HALVES = [slice(0, 64), slice(64, 128)]
QUARTERS = [slice(32 * q, 32 * q + 32) for q in range(4)]


def tile_list_sapline_leak_ledger_kernel(
    tc, tab_words, tab_scales, offs, w1, w2_words, w2_scales, offs2, wgt, sens, w3, w4_words, w4_scales, gain, offs3, wgo, out
):
    nc = tc.nc
    with ExitStack() as ctx:
        keep = ctx.enter_context(tc.tile_pool(name="keep", bufs=1))
        work = ctx.enter_context(tc.tile_pool(name="work", bufs=2))
        psum = ctx.enter_context(tc.psum_pool(name="psum", bufs=4))

        def load_scale_rows(queue, plane, first, rows):
            n = rows.shape[0] * 4
            for q in range(4):
                queue.dma_start(
                    out=plane[32 * q + first : 32 * q + first + n, :].bitcast(I32),
                    in_=rows[:, 4 * q : 4 * q + 4, :].bitcast(I32),
                )

        def deal(dst, src):
            nc.vector.tensor_copy(
                out=dst.rearrange("p (c t m) -> p c m t", t=PACK, m=P),
                in_=src.rearrange("p (c m t) -> p c m t", t=PACK, m=P),
            )

        def load_weight(w, a, c):
            raw = work.tile([P, PACK, BLK], F32, name="raw", tag="raw", bufs=3)
            nc.sync.dma_start(
                out=raw[:], in_=w[BLK * a : BLK * (a + 1), BLK * c : BLK * (c + 1)].rearrange("(p j) n -> p j n", j=PACK)
            )
            return raw

        def round_weight(raw, sign, parts, tag="grouped", bufs=2):
            grouped = work.tile([P, PACK, P, PACK], BF16, name="grouped", tag=tag, bufs=bufs, align_bytes=64)

            def part(ms):
                nc.scalar.activation(
                    out=grouped[:].rearrange("p t m j -> p m j t")[:, ms],
                    in_=raw[:].rearrange("p j (m t) -> p m j t", t=PACK)[:, ms],
                    func=ACT.Copy,
                    scale=sign,
                )

            return grouped, [functools.partial(part, ms) for ms in parts]

        def run(jobs):
            for job in jobs:
                job()

        def quantize(grouped, name):
            codes = keep.tile([P, BLK], U32, name=name + "_codes", align_bytes=64)
            scales = keep.tile([P, BLK], U8, name=name + "_scales", align_bytes=64)
            nc.vector.quantize_mx(out=codes[:].bitcast(FP8X4), scales=scales[:], in_=grouped)
            return codes, scales

        def flat4(grouped):
            return grouped[:].rearrange("p t m j -> p (t m j)")

        def scaled_rows(rows, col, tag, bufs):
            t = work.tile([P, M], F32, name="factor", tag=tag, bufs=bufs)
            nc.scalar.activation(out=t[:], in_=rows[:], func=ACT.Copy, scale=col)
            return t

        list1 = keep.tile([P, S // 16], U16, name="list1")
        list2 = keep.tile([P, M // 16], U16, name="list2")
        list3 = keep.tile([P, M // 16], U16, name="list3")
        tab_s = keep.tile([P, T], U8, name="tab_s", align_bytes=64)
        w2_s_raw = keep.tile([P, BLK], U8, name="w2_s_raw", align_bytes=64)
        late_s_raw = keep.tile([P, N], U8, name="late_s_raw", align_bytes=64)
        v_s = keep.tile([P, S], U8, name="v_s", align_bytes=64)
        nc.vector.memset(tab_s[:].bitcast(I32), 0)
        pages = []
        for k in range(PAGES):
            page = keep.tile([P, T2], F32, name="page%d" % k)
            nc.vector.memset(page[:], 0.0)
            pages.append(page)
        nc.vector.memset(w2_s_raw[:].bitcast(I32), 0)
        nc.vector.memset(late_s_raw[:].bitcast(I32), 0)

        nc.sync.dma_start(list1[:], offs)
        w1_raw0 = load_weight(w1, 0, 0)
        load_scale_rows(nc.sync, tab_s, 0, tab_scales)
        w2_raw = keep.tile([P, 2 * H], U8, name="w2_raw", align_bytes=64)
        nc.sync.dma_start(out=w2_raw[:].bitcast(I32), in_=w2_words[0].bitcast(I32))
        tab_w = keep.tile([P, T], I32, name="tab_w", align_bytes=64)
        nc.sync.dma_start(out=tab_w[:], in_=tab_words[0].rearrange("p t i -> p (t i)").bitcast(I32))
        load_scale_rows(nc.scalar, w2_s_raw, 0, w2_scales[:, :, 0:BLK])
        nc.sync.dma_start(list2[:], offs2)
        wgt_t = keep.tile([P, M], F32, name="wgt_t")
        nc.scalar.dma_start(out=wgt_t[:], in_=wgt)
        sens_t = keep.tile([P, H // BLK, PACK], F32, name="sens_t")
        nc.scalar.dma_start(out=sens_t[:], in_=sens.rearrange("(b p i) -> p b i", p=P, i=PACK))
        w1_raw1 = load_weight(w1, 0, 1)
        load_scale_rows(nc.sync, late_s_raw[:, 0:BLK], 0, w2_scales[:, :, BLK : 2 * BLK])
        load_scale_rows(nc.sync, late_s_raw, 4, w4_scales)

        nc.vector.tensor_copy(v_s[:], tab_s[:].indirect(list1[:]))
        w2_w = keep.tile([P, 2 * H], U8, name="w2_w", align_bytes=64)
        w2_s0 = keep.tile([P, BLK], U8, name="w2_s0", align_bytes=64)
        late_s = keep.tile([P, N], U8, name="late_s", align_bytes=64)
        w2_s = [w2_s0, late_s]
        deal(w2_w[:].bitcast(U16), w2_raw[:].bitcast(U16))
        grouped, jobs = round_weight(w1_raw0, 1.0, HALVES)
        run(jobs)
        w1_q = [quantize(flat4(grouped), "w1_0")]
        deal(w2_s0[:], w2_s_raw[:])
        v_w = []
        for half in range(S // BANK):
            vw = keep.tile([P, BANK], U32, name="v_w%d" % half, align_bytes=64)
            nc.vector.tensor_copy(vw[:], tab_w[:].bitcast(U32).indirect(list1[:, 32 * half : 32 * half + 32]))
            v_w.append(vw)

        w3_q = {}
        x_q = []
        picked = []
        steps = H // P

        w4_raw = []
        for a in range(H // BLK):
            raw4 = keep.tile([P, N], I32, name="w4_raw%d" % a, align_bytes=64)
            w4_raw.append(raw4)
        wgo_t = keep.tile([P, M], F32, name="wgo_t")
        gain_t = keep.tile([P, N // BLK, PACK], F32, name="gain_t")

        def front(step):
            b, i = divmod(step, PACK)
            cols = slice(P * i, P * (i + 1))
            w2_bytes = slice(2 * P * step, 2 * P * (step + 1))
            a_ps, b_ps, th = [], [], []
            h = work.tile([P, S], F32, name="h", tag="h", align_bytes=64)
            for half in range(S // BANK):
                js = slice(BANK * half, BANK * (half + 1))
                pa = psum.tile([P, BANK], F32, name="pa", tag="pa")
                pb = psum.tile([P, BANK], F32, name="pb", tag="pb")
                nc.tensor.matmul_mx(
                    out=pa[:], lhsT=w1_q[b][0][:, cols].bitcast(FP8X4), lhsT_scale=w1_q[b][1][:, cols],
                    rhs=v_w[half][:].bitcast(FP8X4), rhs_scale=v_s[:, js], start=True, stop=True,
                )
                nc.tensor.matmul_mx(
                    out=pb[:], lhsT=w2_w[:, w2_bytes].bitcast(FP4X4), lhsT_scale=w2_s[b][:, cols],
                    rhs=v_w[half][:].bitcast(FP8X4), rhs_scale=v_s[:, js], start=True, stop=True,
                )
                t = work.tile([P, BANK], F32, name="tanh_a", tag="tanh_a", bufs=4)
                nc.scalar.activation(out=t[:], in_=pa[:], func=ACT.Tanh)
                if half == 0 and step > 0:
                    b_sb = work.tile([P, BANK], F32, name="b_sb", tag="b_sb")
                    nc.scalar.copy(out=b_sb[:], in_=pb[:])
                    nc.gpsimd.tensor_tensor(h[:, js], b_sb[:], t[:], ALU.mult)
                a_ps.append(pa)
                b_ps.append(pb)
                th.append(t)
            return a_ps, b_ps, th, h, ws_all[step]

        def gather(step, h, ws):
            b, i = divmod(step, PACK)
            if i == 0:
                picked.append(work.tile([P, PACK, M], F32, name="picked", tag="picked%d" % b, bufs=1, align_bytes=64))
            nc.vector.tensor_tensor(picked[b][:, i, :], h[:].indirect(list2[:]), ws[:], ALU.mult)

        def round_x(b):
            xb = work.tile([P, M, PACK], BF16, name="xb", tag="xb", bufs=1, align_bytes=64)

            def part(copy, cs):
                copy(
                    out=xb[:].rearrange("p (c e) i -> p c i e", e=4)[:, cs],
                    in_=picked[b][:].rearrange("p i (c e) -> p c i e", e=4)[:, cs],
                )

            return xb, part

        def flat3(xb):
            return xb[:].rearrange("p m i -> p (m i)")

        w4_w = []

        def deal_w4(c, tag):
            ww = work.tile([P, H // BLK, BLK], I32, name="w4_w", tag=tag, bufs=1, align_bytes=64)
            for a in range(H // BLK):
                deal(ww[:, a, :], w4_raw[a][:, BLK * c : BLK * (c + 1)])
            w4_w.append(ww)

        ws_all = [scaled_rows(wgt_t, sens_t[:, s // PACK, s % PACK : s % PACK + 1], "ws", steps) for s in range(steps)]
        tiles = {0: front(0)}
        for step in range(steps):
            a_ps, b_ps, th, h, ws = tiles[step]
            lo, hi = h[:, 0:BANK], h[:, BANK:S]
            if step == 0:
                nc.vector.tensor_tensor(lo, b_ps[0][:], th[0][:], ALU.mult)
                nc.vector.tensor_tensor(lo, a_ps[0][:], lo, ALU.max)
            nc.vector.tensor_tensor(hi, b_ps[1][:], th[1][:], ALU.mult)
            if step > 0:
                gather(step - 1, *tiles[step - 1][3:])
            if step == 1:
                deal(late_s[:, 0:BLK], late_s_raw[:, 0:BLK])
            if step == 2:
                w1_q.append(quantize(flat4(g_w1), "w1_1"))
            if step == 4:
                w3_q[0, 0] = quantize(flat4(g_00), "w3_00")
            if step == 5:
                w3_q[1, 0] = quantize(flat4(g_10), "w3_10")
            if step == 6:
                x_q.append(quantize(flat3(xb0), "x0"))
            if step == 7:
                deal_w4(0, "w4_w")
            if step + 1 < steps:
                tiles[step + 1] = front(step + 1)
            if step > 0:
                nc.vector.tensor_tensor(lo, a_ps[0][:], lo, ALU.max)
            nc.vector.tensor_tensor(hi, a_ps[1][:], hi, ALU.max)

            if step == 0:
                g_w1, jobs = round_weight(w1_raw1, 1.0, QUARTERS)
                g_00, more = round_weight(load_weight(w3, 0, 0), -1.0, QUARTERS)
                jobs = jobs + more
                for a in range(H // BLK):
                    nc.sync.dma_start(out=w4_raw[a][:], in_=w4_words[a].rearrange("p n i -> p (n i)").bitcast(I32))
                nc.sync.dma_start(list3[:], offs3)
                nc.sync.dma_start(out=wgo_t[:], in_=wgo)
                nc.sync.dma_start(out=gain_t[:], in_=gain.rearrange("(b p i) -> p b i", p=P, i=PACK))
            if step == 2:
                g_10, more = round_weight(load_weight(w3, 1, 0), -1.0, QUARTERS)
                jobs = jobs + more
            if step == 4:
                xb0, part = round_x(0)
                jobs = jobs + [functools.partial(part, nc.scalar.copy, cs) for cs in QUARTERS]
            run(jobs[:3])
            jobs = jobs[3:]
        g_01, jobs = round_weight(load_weight(w3, 0, 1), -1.0, QUARTERS, "h", 2)
        run(jobs)
        gather(steps - 1, *tiles[steps - 1][3:])
        xb1, part = round_x(1)
        part(nc.scalar.copy, HALVES[0])
        part(nc.vector.tensor_copy, HALVES[1])
        x1_codes = keep.tile([P, M], U32, name="x1_codes", align_bytes=64)
        x1_scales = keep.tile([P, M], U8, name="x1_scales", align_bytes=64)
        m_halves = [slice(M // 2, M), slice(0, M // 2)]
        for ms in m_halves:
            nc.vector.quantize_mx(
                out=x1_codes[:, ms].bitcast(FP8X4), scales=x1_scales[:, ms], in_=xb1[:, ms, :].rearrange("p m i -> p (m i)")
            )
        x_q.append((x1_codes, x1_scales))
        deal_w4(1, "xb")
        deal(late_s[:, BLK:N], late_s_raw[:, BLK:N])
        w3_q[0, 1] = quantize(flat4(g_01), "w3_01")

        out_rows = out.rearrange("(c p i) t -> c i p t", p=P, i=PACK)
        for c in range(N // BLK):
            for i in range(PACK):
                step = PACK * c + i
                cols = slice(P * i, P * (i + 1))
                wg = scaled_rows(wgo_t, gain_t[:, c, i : i + 1], "b_sb", 2)
                if step == 0:
                    sq = work.tile([P, M], F32, name="sq", tag="first_sq", bufs=1, align_bytes=64)
                else:
                    sq = work.tile([P, M], F32, name="sq", tag="sq", bufs=3)
                for k, ms in enumerate(m_halves if step == 0 else [slice(0, M)]):
                    acc = psum.tile([P, ms.stop - ms.start], F32, name="acc", tag=("pb", "pa")[(step + k) % 2])
                    for a in range(H // BLK):
                        nc.tensor.matmul_mx(
                            out=acc[:], lhsT=w3_q[a, c][0][:, cols].bitcast(FP8X4), lhsT_scale=w3_q[a, c][1][:, cols],
                            rhs=x_q[a][0][:, ms].bitcast(FP8X4), rhs_scale=x_q[a][1][:, ms], start=(a == 0), stop=False,
                        )
                        nc.tensor.matmul_mx(
                            out=acc[:], lhsT=w4_w[c][:, a, cols].bitcast(FP8X4), lhsT_scale=late_s[4 + 4 * a : P, BLK * c + P * i : BLK * c + P * (i + 1)],
                            rhs=x_q[a][0][:, ms].bitcast(FP8X4), rhs_scale=x_q[a][1][:, ms], start=False, stop=(a == H // BLK - 1),
                        )
                    nc.scalar.activation(out=sq[:, ms], in_=acc[:], func=ACT.Square)
                page = pages[step % PAGES]
                nc.vector.tensor_tensor(page[:].indirect(list3[:]), sq[:], wg[:], ALU.mult)
                nc.sync.dma_start(out=out_rows[c, i], in_=page[:])
                if step == 0:
                    grouped, jobs = round_weight(load_weight(w3, 1, 1), -1.0, QUARTERS, "first_sq", 1)
                    run(jobs)
                    w3_q[1, 1] = quantize(flat4(grouped), "w3_11")
